import numpy as np, ml_dtypes
CORES = [242,247,114,119]
N = 4
BF = ml_dtypes.bfloat16
def gentries(a):
    return np.ascontiguousarray(a.reshape(8, 16, -1).transpose(0, 2, 1)).reshape(8, -1)
def gtable(e):
    e = np.asarray(e); return np.ascontiguousarray(e.reshape(8, -1, 16).transpose(0, 2, 1)).reshape(128, -1).astype(np.int32)
W, S, ST, HOP = 2048, 256, 3, 1
def sig(v):
    return np.minimum(np.floor(v), 32640).astype(np.float32).astype(BF)
def parts(rng):
    sc = np.exp2(rng.integers(9, 16, (N, 8, 16, 1)).astype(np.float64))
    x = rng.random((N, 8, 16, W)) * sc
    t = np.floor(np.add.reduce(sc, axis=2)[:, :, None, :] * (0.15 + 0.2 * rng.random((N, 8, 16, 1))))
    o = np.argsort(rng.random((N, 8, S)), axis=-1)
    b = np.take_along_axis(o, np.floor(S * rng.random((N, 8, W)) ** 2).astype(np.int64), 2)
    nbr = rng.integers(0, W, (N, 8, 16, W)); L = rng.integers(0, W, (N, 8, S, 16))
    return x, t, b, nbr, L
def plant(rng, b, L):
    n = S // 8
    for q in range(N):
        for g in range(8):
            o = rng.permutation(S); pos = rng.permutation(W)[:3 * n].reshape(n, 3); b[q, g, pos] = o[:n, None]
            rows = np.argsort(rng.random((n, 16)), axis=1)[:, :6]
            L[q, g, o[:n, None], rows] = np.take_along_axis(pos, rng.integers(0, 3, (n, 6)), 1)
            rows = np.argsort(rng.random((n, 16)), axis=1)[:, :6]
            L[q, g, o[n:2 * n, None], rows] = np.take_along_axis(pos[rng.integers(0, n, n)], rng.integers(0, 3, (n, 6)), 1)
            L[q, g, o[2 * n]] = L[q, g, o[2 * n + 1]]; L[q, g, o[2 * n + 2]] = L[q, g, o[2 * n + 3]]
def pack(x, t, b, nbr, L):
    return {"tr": np.stack([gtable(a.reshape(8, -1)) for a in L]), "xs": np.ascontiguousarray(sig(x).reshape(N, 128, W)), "nb": np.ascontiguousarray(nbr.reshape(N, 128, W)).astype(np.int32),
            "lb": np.ascontiguousarray(b).astype(np.int32), "th": np.ascontiguousarray(t.reshape(N, 128, 1)).astype(np.int32)}
def setup_inputs(rng):
    x, t, b, nbr, L = parts(rng); plant(rng, b, L)
    return pack(x, t, b, nbr, L)
def setup_inputs_ties(rng):
    x, t, b, nbr, L = parts(rng)
    unit = rng.choice(np.array([1, 2, 64, 4096]), (N, 8, 1, 1)); unit[:, ::2] = 1
    x = unit * rng.integers(0, 3, (N, 8, 16, W)); x[:, 3] = 0
    t = unit * rng.integers(9, 17, (N, 8, 16, 1))
    b = rng.choice(np.array([0, 1, S // 2, S - 1]), (N, 8, W)); b[:, 1] = rng.integers(0, 24, (N, W)); b[:, 4] = rng.integers(S - 9, S, (N, W))
    return pack(x, t, b, nbr, L)
def setup_inputs_alike(rng):
    x, t, b, nbr, L = parts(rng)
    L[:, 0] = L[:, 0, :1].copy(); L[:, 1] = L[:, 1, :, :1].copy()
    b[:, 2] = 0; b[:, 3] = S - 1
    L[:, 4] = rng.choice(np.array([0, W - 1]), (N, S, 16)); nbr[:, 4] = rng.choice(np.array([0, W - 1, W // 2, 1]), (N, 16, W))
    L[:, 5] = rng.integers(W - 20, W, (N, S, 16))
    for g in (6, 7): L[:, g] = np.arange(S)[None, :, None] + S * rng.integers(0, W // S, (N, S, 16))
    b[:, 6] = np.arange(W) % S; b[:, 7] = (np.arange(W) % S + 1) % S
    return pack(x, t, b, nbr, L)
def setup_inputs_bounds(rng):
    x, t, b, nbr, L = parts(rng); plant(rng, b, L)
    t = np.where(rng.random((N, 8, 16, 1)) < 0.5, rng.choice(np.array([0, 524287]), (N, 8, 16, 1)), t); t[0] = 0; t[1] = 524287
    share = rng.choice(np.array([0.06, 0.3, 0.5, 0.94]), (N, 4, 1, 1))
    x[:, ::2] = np.where(rng.random((N, 4, 16, W)) < share, 32640, 0)
    return pack(x, t, b, nbr, L)
def setup_inputs_far(rng):
    x, t, b, nbr, L = parts(rng); plant(rng, b, L); i = np.arange(S); v = np.arange(W); m = W // S - 1
    low = rng.integers(0, 16, (N, 8, 16, W))
    for g, share in ((0, 0.5), (6, 0.4)):
        x[:, g] = np.where(rng.random((N, 16, W)) < share, 32640, low[:, g]); t[:, g] = rng.integers(200000, 320000, (N, 16, 1))
    for g, n in ((1, 1), (7, 2)):
        x[:, g] = np.where(np.argsort(rng.random((N, 16, W)), axis=1) < n, low[:, g], 32640); t[:, g] = rng.integers(0, 2 ** 17, (N, 16, 1))
    for g in (2, 4, 5):
        L[:, g] = i[None, :, None] + S * rng.integers(0, m, (N, S, 16)); b[:, g] = (v % S + 1) % S
    x[:, 2] = np.where(v < m * S, low[:, 2], 32640)
    np.put_along_axis(L[:, 2], rng.integers(0, 16, (N, S, 1)), i[None, :, None] + m * S, 2)
    t[:, 2] = np.where(rng.random((N, 16, 1)) < 0.5, rng.integers(0, 3, (N, 16, 1)), rng.integers(0, 522241, (N, 16, 1)))
    t[:, 2, 0::4] = rng.integers(393216, 489000, (N, 4, 1)); t[:, 2, 2::4] = rng.integers(327680, 393216, (N, 4, 1))
    t[:, 3] = rng.integers(0, 3, (N, 16, 1)); t[:, 3, ::2] = 0
    a = np.argsort(rng.random((N, W)), axis=1)[:, :S // 2]; L[:, 3, :S // 2] = a[:, :, None]
    np.put_along_axis(b[:, 3], a, (S // 2 + i[:S // 2])[None, :], 1)
    t[:, 4] = rng.integers(0, 3, (N, 16, 1))
    x[:, 5] = np.where(v < m * S, np.where(rng.random((N, 16, W)) < 0.5, 32640, low[:, 5]), rng.integers(15000, 17500, (N, 16, W)))
    nbr[:, 5] = rng.integers(m * S, W, (N, 16, W)); t[:, 5] = rng.integers(489600, 524288, (N, 16, 1))
    return pack(x, t, b, nbr, L)
def setup_inputs_spread(rng):
    x, t, b, nbr, L = parts(rng)
    x = rng.random((N, 8, 16, W)) * np.exp2(15 * rng.random((N, 8, 1, W))) * (rng.random((N, 8, 1, W)) > 0.0625)
    t = np.minimum(np.floor(np.exp2(10 + 9 * rng.random((N, 8, 16, 1)))), 524287)
    b = np.minimum(np.floor(S * rng.random((N, 8, W)) ** 4).astype(np.int64), S - 1)
    L = np.minimum(np.floor(W * rng.random((N, 8, S, 16)) ** 2).astype(np.int64), W - 1)
    plant(rng, b, L)
    return pack(x, t, b, nbr, L)
def check_inputs(d):
    bad = []; v = np.asarray(d["xs"]).astype(np.float32)
    if not (np.all(v == np.floor(v)) and np.min(v) >= 0 and np.max(v) <= 32640): bad.append("whole numbers and range of xs")
    for k, hi in (("tr", W - 1), ("nb", W - 1), ("lb", S - 1), ("th", 524287)):
        if np.min(d[k]) < 0 or np.max(d[k]) > hi: bad.append("range of " + k)
    return bad
def pick(X, c):
    return np.take_along_axis(X, c.reshape(N, 8, 1, S * 16), 3).reshape(N, 8, 16, S, 16)
def reference(tr, xs, nb, lb, th):
    X = xs.astype(np.float32).astype(np.int64).reshape(N, 8, 16, W); near = nb.astype(np.int64).reshape(N, 8, 16, W)
    t = th.astype(np.int64).reshape(N, 8, 1, 16); b = lb.astype(np.int64); i = np.arange(S)
    L = np.stack([gentries(a) for a in tr]).astype(np.int64).reshape(N, 8, S, 16)
    for st in range(ST):
        x = pick(X, L); y = np.add.reduce(x, axis=4) >> 4
        E = np.add.reduce(np.abs(x - y[..., None]), axis=2)
        p = np.take_along_axis(L, np.argmin(E, axis=3)[..., None], 3)[..., 0]
        v = np.take_along_axis(b, L.reshape(N, 8, S * 16), 2).reshape(N, 8, S, 16)
        votes = np.add.reduce((v[..., :, None] == v[..., None, :]).astype(np.int64), axis=4)
        H = np.take_along_axis(v, np.argmax(votes, axis=3)[..., None], 3)[..., 0]
        child = (H[..., :, None] == i) & (i[:, None] != i)
        don = np.min(np.where(child, i[:, None], S), axis=2); d0 = np.minimum(don, S - 1)[..., None]
        Ld = np.take_along_axis(L, d0, 2); Ed = np.take_along_axis(E, d0, 2)
        fill = np.take_along_axis(near, p[:, :, None, :], 3).swapaxes(2, 3)
        c = np.where((don < S)[..., None] & (Ed > t), Ld, fill)
        F = np.add.reduce(np.abs(pick(X, c) - y[..., None]), axis=2)
        new = np.where(F < E, c, L)
        again = np.argmax(p[..., :, None] == p[..., None, :], axis=3) < i
        new = np.where(again[..., None], fill, new)
        bb = np.concatenate([b, np.zeros((N, 8, 1), np.int64)], axis=2)
        np.put_along_axis(bb, np.where(again, W, p), np.broadcast_to(i, (N, 8, S)), 2); b = bb[..., :W]
        L = np.roll(new, HOP, axis=0) if st < ST - 1 else new
    return {"yl": np.stack([gtable(a.reshape(8, -1)) for a in L]).astype(np.float32), "yb": np.ascontiguousarray(b).astype(np.float32)}

import numpy as np
from concourse.mybir import AluOpType as A, ActivationFunctionType as F, AxisListType as AX

SCRATCH = {}
for _d, _l in (
    ("bfloat16", "xs2 4096 lbw 2560 lbc 128 gx 4096 gv 4096 gcd 4096 eqb 2176 absb 2176 eqv 2048 V2 368 te 16 prepH 256 nd 256 "
                 "Ib 128 Ib16 128 Ib4k 128 Ib2k 128 c75 128 Bx 8 BV 8 thr 256 Wt 128 Wo 128 jrow 256"),
    ("float32", "thf 16 mE 4096 mF 4096 L2 256 ysb 256 ytm 256 tA 128 t1 128 t2 64 t3 32 t4 16 tq 16 PlH 16 PlP 16 fl 256 fm 16 "
                "oH 16 oP 16 oS 16 oHm 16 oPm 16 m1 256 G 256 d1 256 Us 256 keyS 256 Ld 512 cp 256 tk 256 w2 512 outf 256 one 144 If 128 "
                "blk0 128 blk 128 By 128 Bm 8 hc0 16 hc 16 rst 128 rsn 256 hf0 32 kf 256 thrf 256 pm 16 i16 16 b16 16 wm 16 wc 16 dH 16 dP 16 dS 16"),
    ("float16", "td 16 Lh 256 Ih 128 Ifn 128 Ifs 128 Ifb 128 s2 256 tm 256 prep 256"),
    ("int32", "nbw 2048 lbi 128 tri 256 pi 16 pa 16 thi 16"),
    ("uint16", "L0 256 uH 16 uP 16 uL 16 uS 16 cu 256 in10 128 in11 128 in20 128 in21 128 snd10 128 snd11 128 snd20 128 snd21 128")):
    _w = _l.split()
    for _i in range(0, len(_w), 2):
        SCRATCH[_w[_i]] = ("sbuf", [128, int(_w[_i + 1])], _d)
for _n, _p, _c, _d in (("rTH", 8, 256, "bfloat16"), ("rTP", 8, 256, "float16"), ("W8f", 8, 144, "float32"), ("W8", 8, 144, "float16"),
                       ("W8b", 8, 144, "bfloat16"), ("Rp0", 8, 128, "float32"), ("Rep", 8, 128, "float16"), ("Repb", 8, 128, "bfloat16"),
                       ("oneb", 2, 128, "bfloat16"), ("krow", 1, 128, "bfloat16"), ("c1k", 1, 128, "bfloat16"), ("vrow", 2, 256, "bfloat16")):
    SCRATCH[_n] = ("sbuf", [_p, _c], _d)
for _b in range(8):
    SCRATCH["B%d" % _b] = ("psum", [128, 512], "float32")
SEMAPHORES = ["sv", "ss", "st", "sg", "sent", "a10", "a11", "a20", "a21"] + ["d%d" % _i for _i in range(12)]

CY = np.array([1.04, 1.0, 1.1]); OV = np.array([40.0, 30.0, 50.0]); GA = np.array([1.56, 1.15, 1.95]); SC = np.array([3.8, 2.5, 5.0])
PCY = np.array([0.52, 0.7, 0.42]); LAT = np.array([110.0, 80.0, 150.0]); SLAT = np.array([70.0, 50.0, 100.0]); LINK = np.array([2500.0, 2000.0, 3500.0])
ONE = np.ones(3)
TRIES, SEED, FB, CP, TEMP = 8000, 1, 0.2, 0.6, 500.0
OPT = {"R": 4, "Q": 8, "H": ((0, 2, 1), (2, 5, 0), (5, 9, 0), (9, 16, 0)), "P0": ((0, 8, 1),), "P1": ((0, 8, 0), (8, 16, 0))}
SEM = {"v": "sv", "s": "ss", "t": "st", "g": "sg"}
CACHE = {}


def isfn(x):
    return str(x).startswith("<function")


def vcall(g, name, a):
    v = g.vector
    if name == "memset": return v.memset(*a)
    if name == "copy": return v.tensor_copy(*a)
    if name == "tt": return v.tensor_tensor(*a)
    if name == "scan": return v.tensor_tensor_scan(*a)
    if name == "red": return v.tensor_reduce(*a)
    return v.tensor_scalar(*a)


def build():
    ops = []
    lastw, readers, bank_ops, bank_pe = {}, {}, {}, {}
    ndma = [0]; cur = [-1]; grp = []

    def op(eng, fn, r, w, cost, banks=(), kind="c", lat=0.0, sem=None, alt=None):
        i = len(ops)
        hard, soft = set(), set()
        for x in r:
            if x in lastw: hard.add(lastw[x])
        for x in w:
            if x in lastw: hard.add(lastw[x])
            for j in readers.get(x, ()): hard.add(j)
        for b in banks:
            for j in bank_ops.get(b, ()):
                if ops[j]["eng"] != eng or alt or ops[j]["alt"]: hard.add(j)
            if eng == "t" and b in bank_pe: soft.add(bank_pe[b])
        if eng == "t":
            pe = set(j for j in hard if ops[j]["eng"] == "t"); hard -= pe; soft |= pe
        for x in r: readers.setdefault(x, []).append(i)
        for x in w: lastw[x] = i; readers[x] = []
        for b in banks:
            bank_ops.setdefault(b, []).append(i)
            if eng == "t": bank_pe[b] = i
        hard.discard(i)
        ops.append(dict(eng=eng, fn=fn, hard=hard, soft=soft, cost=cost * ONE, kind=kind, lat=lat * ONE, sem=sem, w=w, alt=alt, st=cur[0]))

    def vc(n): return max(64, n) * CY + OV if isinstance(n, int) else n
    def gcost(n): return 60 + n * GA * CY
    def scost(n): return 60 + n * SC * CY
    def V(name, r, w, n, banks, *a):
        op("v", lambda g, T: vcall(g, name, [x(T) if isfn(x) else x for x in a]), r, w, vc(n), banks)
    def S(r, w, n, banks, out, in_, func, bias=None, scale=None):
        def fn(g, T):
            kw = {}
            if bias is not None: kw["bias"] = bias(T) if isfn(bias) else bias
            if scale is not None: kw["scale"] = scale(T) if isfn(scale) else scale
            return g.scalar.activation(out(T), in_(T), func, **kw)
        op("s", fn, r, w, vc(n), banks)
    def either(r, w, c, out, src, banks=(), add=None):
        if add is None:
            op("s", lambda g, T: g.scalar.activation(out(T), src(T), F.Copy), r, w, vc(c), banks, alt=lambda g, T: g.vector.tensor_copy(out(T), src(T)))
        else:
            op("s", lambda g, T: g.scalar.activation(out(T), src(T), F.Identity, bias=add), r, w, vc(c), banks,
               alt=lambda g, T: g.vector.tensor_scalar(out(T), src(T), add, None, A.add))
    def M(r, w, bank, out, l, rhs, st, sp, m, n, f32=False, more=False):
        grp.append((r, out, l, rhs, st, sp, max(min(64, m), n) * (4 if f32 else 1) * PCY + 4))
        if more: return
        gs = list(grp); del grp[:]
        def fn(g, T):
            for e in gs: ins = g.tensor.matmul(e[1](T), e[2](T), e[3](T), e[4], e[5])
            return ins
        op("t", fn, [x for e in gs for x in e[0]], w, sum(e[6] for e in gs), [bank])
    def D(q, out, in_, r, w, lat):
        s = "d%d" % ndma[0]; ndma[0] += 1
        def fn(g, T):
            e = g.sync if q == "y" else (g.scalar if q == "s" else g)
            return e.dma_start(out(T), in_(T))
        op(q, fn, r, w, 60 if q != "g" else 1000, kind="d", lat=lat, sem=s)
    def P(name, r, w, n, *a, **kw):
        def fn(g, T):
            b = [x(T) if isfn(x) else x for x in a]
            return g.iota(*b, **kw) if name == "iota" else g.affine_select(*b)
        op("g", fn, r, w, 170 + n * CY * 2)
    def ap(n, *ix):
        if len(ix) == 0: return lambda T: T[n][:]
        if len(ix) == 1: return lambda T: T[n][:, ix[0]]
        return lambda T: T[n][ix[0], ix[1]]
    def ind(n, a, b, o, c, d): return lambda T: T[n][:, a:b].indirect(T[o][:, c:d])
    def hq(x, hf): return [(x, 4 * hf + q) for q in range(4)]
    def h_(hf): return slice(128 * hf, 128 * hf + 128)
    s_ = slice; YB = ("B1", "B6"); p8 = s_(0, 8); ID = F.Identity; R = OPT["R"]
    fl = dict(allow_small_or_imprecise_dtypes=True)

    D("y", ap("tri"), ap("tr"), [], ["tri"], 2200)
    D("y", ap("xs2", s_(0, 2048)), ap("xs"), [], ["xsa"], 3000)
    D("s", ap("lbi"), ap("lb"), [], ["lbi"], 2000)
    D("y", ap("thi", s_(0, 1)), ap("th"), ["tri"], ["thi"], 2500)
    D("y", ap("xs2", s_(2048, 4096)), ap("xs"), ["tri"], ["xsb"], 5000)
    D("y", ap("nbw"), ap("nb"), ["tri"], ["nbw"], 8000)
    V("memset", [], ["lbw"], 1024, [], ap("lbw", s_(0, 2048)), 0.0)
    V("copy", ["lbi"], ["lbc"], 128, [], ap("lbc"), ap("lbi"))
    D("y", ap("lbw", s_(0, 128, 16), s_(0, 2048)), ap("lbc"), ["lbc"], ["lbw"], 2200)
    V("ts", ["thi"], ["thf"], 16, [], ap("thf", s_(0, 1)), ap("thi", s_(0, 1)), -16.0, -0.5, A.mult, A.add)
    V("memset", [], ["one"], 144, [], ap("one"), 1.0)
    P("sel", ["one"], ["If"], 128, ap("If"), ap("one", s_(0, 128)), [[-1, 128]], A.is_equal, 0.0, 0, 1)
    for n, c in (("Ib16", 1 / 16), ("Ib", 1.0), ("Ib4k", 4096.0), ("Ib2k", -1024.0)):
        S(["If"], [n], 128, [], ap(n), ap("If"), ID, scale=c)
    for n, c in (("Ifs", 1 / 2048), ("Ifb", 2048.0), ("Ifn", -1.0), ("Ih", 1.0)):
        V("ts", ["If"], [n], 128, [], ap(n), ap("If"), c, None, A.mult)
    V("memset", [], ["c75"], 64, [], ap("c75"), -7.5)
    P("sel", ["one"], ["blk0"], 128, ap("blk0"), ap("one", s_(0, 128)), [[-16, 8], [0, 16]], A.is_ge, 0.0, 0, 1)
    P("sel", ["blk0"], ["blk"], 128, ap("blk"), ap("blk0"), [[16, 8], [0, 16]], A.is_ge, 0.0, 15, -1)
    S(["blk"], ["By"], 128, [], ap("By"), ap("blk"), ID, scale=-16.0)
    S(["blk"], ["Bm"], 8, [], ap("Bm"), ap("blk", s_(0, 128, 16)), ID, scale=32.0)
    S(["blk"], ["Bx"], 8, [], ap("Bx"), ap("blk", s_(0, 128, 16)), ID, scale=-16.0)
    S(["If"], ["BV"], 8, [], ap("BV"), ap("If", s_(0, 128, 16)), F.Copy)
    P("sel", ["one"], ["W8f"], 144, ap("W8f"), ap("one", p8, s_(0, 144)), [[-1, 144]], A.is_equal, 0.0, 15, 16)
    V("copy", ["W8f"], ["W8"], 144, [], ap("W8"), ap("W8f"))
    S(["W8f"], ["W8b"], 144, [], ap("W8b"), ap("W8f"), F.Copy)
    P("sel", ["one"], ["Rp0"], 128, ap("Rp0"), ap("one", p8, s_(0, 128)), [[-1, 8], [0, 16]], A.is_equal, 0.0, 0, 1)
    V("copy", ["Rp0"], ["Rep"], 128, [], ap("Rep"), ap("Rp0"))
    S(["Rp0"], ["Repb"], 128, [], ap("Repb"), ap("Rp0"), F.Copy)
    P("iota", [], ["c1k"], 128, ap("c1k"), [[0, 128]], -1024, 0, **fl)
    V("memset", [], ["oneb"], 64, [], ap("oneb"), 1.0)
    P("iota", [], ["krow"], 128, ap("krow"), [[0, 8], [1, 16]], 0, 0, **fl)
    V("memset", [], ["vrow"], 128, [], ap("vrow"), -127.5)
    P("iota", [], ["vrow"], 256, ap("vrow", s_(0, 1), s_(0, 256)), [[-256, 16], [0, 16]], 3840, 0, **fl)
    P("iota", [], ["hc0"], 16, ap("hc0"), [[128, 2], [0, 8]], 0, 1, **fl)
    S(["hc0"], ["hc"], 16, [], ap("hc"), ap("hc0"), ID, bias=-127.5)
    P("iota", [], ["kf"], 256, ap("kf"), [[0, 16], [1, 16]], 0, 0, **fl)
    V("ts", ["kf"], ["rsn"], 256, [], ap("rsn"), ap("kf"), 0.0, -1e20, A.is_equal, A.mult)
    S(["rsn"], ["rst"], 128, [], ap("rst"), ap("rsn", s_(0, 128)), ID, scale=-1.0)
    P("iota", [], ["pi"], 16, ap("pi"), [[0, 16]], 0, 1)
    V("ts", ["pi"], ["pa"], 16, [], ap("pa"), ap("pi"), 15, None, A.bitwise_and)
    V("copy", ["pa"], ["pm"], 16, [], ap("pm"), ap("pa"))
    P("iota", [], ["i16"], 16, ap("i16"), [[1, 16]], 0, 0, **fl)
    V("memset", [], ["hf0"], 16, [], ap("hf0", s_(0, 16)), 0.5)
    V("scan", ["hf0"], ["pw"], 16, [], ap("hf0", s_(16, 32)), ap("hf0", s_(0, 16)), ap("hf0", s_(0, 16)), 2.0 ** 29, A.mult, A.max)
    V("tt", ["i16", "pm"], ["wm"], 32, [], ap("wm"), ap("i16"), ap("pm"), A.is_equal)
    V("tt", ["wm", "pw"], ["b16"], 32, [], ap("b16"), ap("wm"), ap("hf0", s_(16, 32)), A.mult)
    V("red", ["b16"], ["wc"], 16, [], ap("wc", s_(0, 1)), ap("b16"), AX.X, A.add)
    S(["blk", "wc"], ["Wt"], 128, [], ap("Wt"), ap("blk"), ID, scale=ap("wc", s_(0, 1)))
    S(["blk"], ["Wo"], 128, [], ap("Wo"), ap("blk"), ID, scale=2.0 ** 29)
    V("ts", ["kf", "pm"], ["thrf"], 256, [], ap("thrf"), ap("kf"), ap("pm", s_(0, 1)), -2.0 ** 40, A.not_equal, A.mult)
    S(["wc"], ["wc2"], 16, [], ap("wc", s_(4, 5)), ap("wc", s_(0, 1)), ID, scale=-2.0)
    S(["thrf", "wc2"], ["thr"], 256, [], ap("thr"), ap("thrf"), ID, bias=ap("wc", s_(4, 5)))
    V("ts", ["i16", "pm"], ["wm"], 16, [], ap("wm"), ap("i16"), 16.0, ap("pm", s_(0, 1)), A.mult, A.add)
    for n, c in (("dH", 256.0 - 4096), ("dP", 2304.0 - 4096), ("dS", 2048.0 - 4096)):
        S(["wm"], [n], 16, [], ap(n), ap("wm"), ID, bias=c)
    P("iota", [], ["jrow"], 256, ap("jrow"), [[1, 256]], 0, 0, **fl)

    def gather(name, win, wa, wb, wres, offs):
        d = 8 // OPT["Q"]
        for q in range(0, 8, d):
            o, c0, res = offs(q)
            either(wres + [res], [(name, q + e) for e in range(d)], gcost(512 * d), ap(name, s_(512 * q, 512 * (q + d))), ind(win, wa, wb, o, c0, c0 + 32 * d))

    def energy(x, m, hf, first):
        B = "B%d" % (2 + hf); key = ("key", hf); K = ap(B, s_(0, 128)); a = 2048 * hf; c = 16 // R
        if first:
            M(["oneb", "krow"], [key], B, K, ap("oneb", s_(0, 1), s_(0, 128)), ap("krow"), True, False, 128, 128)
        else:
            M([("ysb", hf), "By"], [key], B, K, ap("ysb", h_(hf)), ap("By"), True, False, 128, 128, True)
        for k in range(16):
            M(hq(x, hf) + ["Bx"], [key], B, ap(B, s_(k, 128, 16)), ap(x, s_(a + k, a + 2048, 16)), ap("Bx"), False, False, 128, 8, more=k % 8 < 7)
        if first:
            M([("ysb", hf), "By"], [key], B, K, ap("ysb", h_(hf)), ap("By"), False, False, 128, 128, True)
        for k in range(c):
            V("tt", hq(x, hf) + [("y2", hf, e) for e in range(R)], [(m, hf, k)], 128 * R, [YB[hf]], ap(m, s_(a + k, a + 2048, c)),
              ap(x, s_(a + k, a + 2048, c)), ap(YB[hf], s_(0, 128 * R)), A.max)
        for k0 in range(c):
            for k in range(k0, 16, c):
                M([(m, hf, k0), "Bm"], [key], B, ap(B, s_(k, 128, 16)), ap(m, s_(a + k, a + 2048, 16)), ap("Bm"), False, k == 15, 128, 8, True, more=k < 16 - c)

    def repeats(nm, c0, c1, rres, pres, groups):
        rT, Pl, prep, Rep, dummy, o = ("rTH", "PlH", "prepH", "Repb", "dH", "oH") if nm == "H" else ("rTP", "PlP", "prep", "Rep", "dP", "oP")
        t = (nm, c0); l = s_(c0 // 16, c1 // 16); nb = c1 // 16; e0 = 0 if c0 == 0 else 576
        def PP(u, v): return ap("B4", s_(256 + u, 256 + v))
        def TT(u, v): return ap("B5", s_(256 + u, 256 + v))
        def each(n): return [(n, c) for c in range(c0, c1, 128)]
        pp, tt_ = each("prepP"), each("TT")
        M(rres + [Rep], pp, "B4", PP(c0, c1), ap(Rep), ap(rT, s_(c0, c1)), True, True, 128, c1 - c0)
        if not all(x[2] for x in groups):
            if nm == "H": either(pp, [("prep", t)], c1 - c0, ap(prep, s_(c0, c1)), PP(c0, c1), ["B4"])
            else: V("copy", pp, [("prep", t)], c1 - c0, ["B4"], ap(prep, s_(c0, c1)), PP(c0, c1))
        M(["Ib", "thr"], tt_, "B5", TT(c0, c1), ap("Ib"), ap("thr", s_(c0, c1)), True, False, 128, c1 - c0)
        lo = [max(16 * b, c0) for b in range(nb)]
        c_ = [e0 + sum(c1 - lo[c] for c in range(b)) for b in range(nb + 1)]
        def eb(n, b): return [(n, c // 16) for c in range(c_[b], c_[b + 1], 16)]
        for b0, b1, act in groups:
            for b in range(b0, b1):
                if act: S(pp + pres, eb("absb", b), c1 - lo[b], ["B4"], ap("absb", s_(c_[b], c_[b + 1])), PP(lo[b], c1), F.Abs, bias=ap(Pl, s_(b, b + 1)), scale=-1.0)
                else: V("ts", [("prep", t)] + pres, eb("eqb", b), (c1 - lo[b]) // 2, [], ap("eqb", s_(c_[b], c_[b + 1])), ap(prep, s_(lo[b], c1)),
                        ap(Pl, s_(b, b + 1)), None, A.is_equal)
            if act: S([x for b in range(b0, b1) for x in eb("absb", b)], [x for b in range(b0, b1) for x in eb("eqb", b)], c_[b1] - c_[b0], [],
                      ap("eqb", s_(c_[b0], c_[b1])), ap("absb", s_(c_[b0], c_[b1])), F.Relu, bias=1.0, scale=-1.0)
            for b in range(b0, b1):
                d = 16 if 16 * b >= c0 else 0; last = b == nb - 1
                if d: M(eb("eqb", b) + ["Wt"], tt_, "B5", TT(16 * b, 16 * b + 16), ap("Wt"), ap("eqb", s_(c_[b], c_[b] + 16)), False, last, 128, 16, more=not last)
                if not last:
                    M(eb("eqb", b) + ["Wo"], tt_, "B5", TT(lo[b] + d, c1), ap("Wo"), ap("eqb", s_(c_[b] + d, c_[b + 1])), False, False, 128, c1 - lo[b] - d,
                      more=b % 2 == 0 and b + 1 < b1)
        either(pres, [("om", t)], 16, ap(o + "m", l), ap(Pl, l), add=-4096.0)
        V("scan", tt_ + ["rsn"], each("fl"), c1 - c0, ["B5"], ap("fl", s_(c0, c1)), ap("rsn", s_(c0, c1)), TT(c0, c1), 0.0, A.add, A.max)
        V("tt", each("fl") + [("om", t)], each("fm"), 32, [], ap("fm", l), ap("fl", s_(c0 + 15, c1, 16)), ap(o + "m", l), A.max)
        V("tt", each("fm") + [dummy], [("o", t)], 32, [], ap(o, l), ap("fm", l), ap(dummy, l), A.min)

    def cores(c0, c1, groups):
        hs = range(c0 // 128, c1 // 128); l = s_(c0 // 16, c1 // 16); t = ("P", c0)
        repeats("P", c0, c1, [("rTP", h) for h in hs], [("PlP", h) for h in range(c1 // 128)], groups)
        V("ts", [("o", t)], [("uL", c0)], 16, [], ap("uL", l), ap("oP", l), 4096.0, None, A.add)
        V("tt", [("o", t), "dS"], [("oS", c0)], 32, [], ap("oS", l), ap("oP", l), ap("dS", l), A.max)
        V("ts", [("oS", c0)], [("uS", h) for h in hs], 16, [], ap("uS", l), ap("oS", l), 2048.0, None, A.add)
        V("copy", [("uL", c0), "jrow"], ["lbw"], scost(c1 - c0), [], ind("lbw", 0, 2560, "uL", c0 // 16, c1 // 16), ap("jrow", s_(c0, c1)))

    MAG, MAG2 = 12582912.0, 3221225472.0
    for st in range(3):
        cur[0] = st
        if st == 0:
            V("copy", ["tri"], [("Lu", 0), ("Lu", 1)], 256, [], ap("L0"), ap("tri"))
            V("copy", ["tri"], [("Lh", 0), ("Lh", 1)], 256, [], ap("Lh"), ap("tri"))
            offs = lambda q: ("L0", 32 * q, ("Lu", q // 4))
        else:
            for hf in (0, 1):
                V("copy", [("in", st, hf)], [("Lh", hf)], 64, [], ap("Lh", h_(hf)), ap("in%d%d" % (st, hf)))
            offs = lambda q, st=st: ("in%d%d" % (st, q // 4), 32 * (q % 4), ("in", st, q // 4))
        P("iota", [], ["Ld"], 256, ap("Ld", s_(0, 256)), [[0, 256]], -1, 0, **fl)
        for hf in (0, 1):
            B = "B%d" % (2 + hf); N_ = ap(B, s_(384, 512))
            M([("Lh", hf), "Ih"], [("np", hf)], B, N_, ap("Ih"), ap("Lh", h_(hf)), True, True, 128, 128)
            either([("np", hf)], [("L2", hf)], 128, ap("L2", h_(hf)), N_, [B], add=2048.0)
            M([("Lh", hf), "Ifs"], [("LT", hf)], B, ap(B, s_(128, 256)), ap("Lh", h_(hf)), ap("Ifs"), True, True, 128, 128)
        gather("gv", "lbw", 0, 2048, ["lbw"], offs)
        gather("gx", "xs2", 0, 2048, ["xsa"], offs)
        for hf in (0, 1):
            H = h_(hf); Y = YB[hf]
            M(["Ib16", "c75"], [("S", hf)], "B0", ap("B0", H), ap("Ib16"), ap("c75"), True, False, 128, 128)
            for k in range(16):
                M(hq("gx", hf) + ["Ib16"], [("S", hf)], "B0", ap("B0", H), ap("Ib16"),
                  ap("gx", s_(2048 * hf + k, 2048 * hf + 2048, 16)), False, k == 15, 128, 128, more=k % 8 < 7)
            either([("S", hf)], [("ytm", hf)], 128, ap("ytm", H), ap("B0", H), ["B0"], add=MAG)
            for e in range(R):
                either([("ytm", hf)], [("y2", hf, e)], 128, ap(Y, s_(e, 128 * R, R)), ap("ytm", H), [Y], add=-MAG)
            either([("ytm", hf)], [("ysb", hf)], 128, ap("ysb", H), ap("ytm", H), add=-MAG)
        for hf in (0, 1):
            for k in range(16):
                M(hq("gv", hf) + ["BV"], ["VT"], "B4", ap("B4", s_(16 * k + 8 * hf, 16 * k + 8 * hf + 8)),
                  ap("gv", s_(2048 * hf + k, 2048 * hf + 2048, 16)), ap("BV"), True, True, 128, 8, more=k < 15)
        either(["VT"], ["V2a"], 256, ap("V2", s_(0, 256)), ap("B4", s_(0, 256)), ["B4"])
        either(["VT"], ["V2b"], 112, ap("V2", s_(256, 368)), ap("B4", s_(0, 112)), ["B4"])
        M(["oneb", "vrow"], ["K2"], "B5", ap("B5", s_(0, 256)), ap("oneb"), ap("vrow"), True, False, 128, 256)
        M(["Ib", "V2a"], ["K2"], "B5", ap("B5", s_(0, 256)), ap("Ib"), ap("V2", s_(0, 256)), False, False, 128, 256)
        for s in range(1, 9):
            n = 256 if s < 8 else 128; a = 256 * (s - 1); u = 256 - 16 * s
            V("tt", ["VT", "V2a", "V2b"], [("eqv", s)], n, ["B4"], ap("eqv", s_(a, a + n)), ap("B4", s_(0, n)), ap("V2", s_(16 * s, 16 * s + n)), A.is_equal)
            M([("eqv", s), "Ib4k"], ["K2"], "B5", ap("B5", s_(0, u)), ap("Ib4k"), ap("eqv", s_(a, a + u)), False, s == 8, 128, u, more=s < 8)
            if s < 8:
                M([("eqv", s), "Ib4k"], ["K2"], "B5", ap("B5", s_(0, 16 * s)), ap("Ib4k"), ap("eqv", s_(a + u, a + 256)), False, False, 128, 16 * s)
        either(["K2"], ["tA"], 128, ap("tA"), ap("B5", s_(128, 256)), ["B5"])
        V("tt", ["K2", "tA"], ["t1"], 128, ["B5"], ap("t1"), ap("B5", s_(0, 128)), ap("tA"), A.max)
        V("tt", ["t1"], ["t2"], 128, [], ap("t2"), ap("t1", s_(0, 64)), ap("t1", s_(64, 128)), A.max)
        V("tt", ["t2"], ["t3"], 64, [], ap("t3"), ap("t2", s_(0, 32)), ap("t2", s_(32, 64)), A.max)
        V("tt", ["t3"], ["t4"], 32, [], ap("t4"), ap("t3", s_(0, 16)), ap("t3", s_(16, 32)), A.max)
        V("ts", ["t4"], ["tq"], 16, [], ap("tq"), ap("t4"), MAG2, MAG2, A.add, A.subtract)
        V("tt", ["t4", "tq"], ["td"], 32, [], ap("td"), ap("t4"), ap("tq"), A.subtract)
        V("tt", ["td", "hc"], ["te"], 32, [], ap("te"), ap("td"), ap("hc"), A.is_equal)
        for hf in (0, 1):
            M(["td", "Ih", "t1"], ["rTHp"], "B5", ap("B5", p8, h_(hf)), ap("td", s_(8 * hf, 8 * hf + 8)), ap("Ih"), True, False, 8, 128, more=True)
            M(["te", "Ib4k"], ["rTHp"], "B5", ap("B5", p8, h_(hf)), ap("te", s_(8 * hf, 8 * hf + 8)), ap("Ib4k"), False, True, 8, 128, more=hf == 0)
        either(["rTHp"], ["rTH"], 256, ap("rTH"), ap("B5", p8, s_(0, 256)), ["B5"], add=127.5)
        for jl in range(16):
            M(["rTH", "W8b"], ["lH"], "B7", ap("B7", s_(288, 304)), ap("W8b", s_(15 - jl, 143 - jl)), ap("rTH", s_(jl, 256, 16)), jl == 0, jl == 15, 128, 16, more=jl < 15)
        either(["lH"], ["PlH"], 16, ap("PlH"), ap("B7", s_(288, 304)), ["B7"])
        repeats("H", 0, 256, ["rTH"], ["PlH"], OPT["H"])
        V("ts", [("o", ("H", 0))], ["uH"], 16, [], ap("uH"), ap("oH"), 4096.0, None, A.add)
        for hf in (0, 1):
            B = "B%d" % (2 + hf); key = ("key", hf); K = ap(B, s_(0, 128)); H = h_(hf)
            energy("gx", "mE", hf, True)
            either([key], [("keyS", hf)], 128, ap("keyS", H), K, [B], add=-15.0)
            V("scan", [key, "rst"], [("m1", hf)], 128, [B], ap("m1", H), ap("rst"), K, 0.0, A.add, A.min)
            V("tt", [key, ("m1", hf)], [("G", hf)], 128, [B], ap("G", H), K, ap("m1", H), A.subtract)
            V("tt", [("LT", hf), ("G", hf)], [("d1", hf)], 128, [B], ap("d1", H), ap(B, s_(128, 256)), ap("G", H), A.subtract)
            V("scan", [("G", hf), ("d1", hf)], [("s2", hf)], 128, [], ap("s2", H), ap("G", H), ap("d1", H), 0.0, A.min, A.max)
            M([("keyS", hf), "If"], [("U", hf)], "B7", ap("B7", H), ap("keyS", H), ap("If"), True, True, 128, 128, True)
            S([("U", hf), "thf"], [("Us", hf)], 128, ["B7"], ap("Us", H), ap("B7", H), F.Sign, bias=ap("thf", s_(0, 1)))
            V("tt", [("Us", hf), ("L2", hf), "uH"], ["Ld"], scost(128), [], ind("Ld", 0, 512, "uH", 8 * hf, 8 * hf + 8), ap("Us", H), ap("L2", H), A.mult)
            RP = ap("B0", p8, s_(256 + 128 * hf, 384 + 128 * hf))
            M([("s2", hf), "Ifb"], [("rTPp", hf)], "B0", RP, ap("s2", s_(128 * hf + 15, 128 * hf + 128, 16)), ap("Ifb"), True, True, 8, 128)
            V("copy", [("rTPp", hf)], [("rTP", hf)], 128, ["B0"], ap("rTP", H), RP)
            c8 = s_(256 + 8 * hf, 264 + 8 * hf); o8 = s_(8 * hf, 8 * hf + 8)
            for jl in range(16):
                M([("rTP", hf), "W8"], [("lP", hf)], "B7", ap("B7", c8), ap("W8", s_(15 - jl, 143 - jl)), ap("rTP", s_(128 * hf + jl, 128 * hf + 128, 16)),
                  jl == 0, jl == 15, 128, 8, more=jl < 15)
            V("copy", [("lP", hf)], [("uP", hf)], 8, ["B7"], ap("uP", o8), ap("B7", c8))
            either([("lP", hf)], [("PlP", hf)], 8, ap("PlP", o8), ap("B7", c8), ["B7"])
            if hf == 0: cores(0, 128, OPT["P0"])
        for hf in (0, 1):
            H = h_(hf)
            V("tt", ["nbw", ("uP", hf), "Ld"], [("cp", hf)], gcost(128), [], ap("cp", H), ind("nbw", 0, 2048, "uP", 8 * hf, 8 * hf + 8), ap("Ld", H), A.max)
            V("copy", [("cp", hf)], [("cu", hf)], 128, [], ap("cu", H), ap("cp", H))
        S(["Ld"], ["nd"], 256, [], ap("nd"), ap("Ld", s_(0, 256)), F.Sign)
        gather("gcd", "xs2", 0, 4096, ["xsa", "xsb"], lambda q: ("cu", 32 * q, ("cu", q // 4)))
        for hf in (0, 1):
            B = "B%d" % (2 + hf); H = h_(hf); E = ap(B, s_(256, 384))
            M([("cp", hf), "If"], [("e1", hf)], B, E, ap("cp", H), ap("If"), True, False, 128, 128, True)
            M([("Lh", hf), "Ifn"], [("e1", hf)], B, E, ap("Lh", H), ap("Ifn"), False, False, 128, 128, more=True)
            M(["nd", "Ib2k"], [("e1", hf)], B, E, ap("nd", H), ap("Ib2k"), False, False, 128, 128, more=True)
            M(["oneb", "c1k"], [("e1", hf)], B, E, ap("oneb", s_(0, 1), s_(0, 128)), ap("c1k"), False, True, 128, 128)
        cores(128, 256, OPT["P1"])
        V("copy", ["nbw", ("uP", 0), ("uP", 1)], ["w2f"], gcost(256), [], ap("w2", s_(256, 512)), ind("nbw", 0, 2048, "uP", 0, 16))
        if st == 0:
            V("memset", [], [("w2", 1)], 128, [], ap("w2", h_(1)), 0.0)
        if st == 2:
            D("g", ap("yb"), ap("lbw", s_(0, 128, 16), s_(0, 2048)), ["lbw"], ["yb"], 2500)
        for hf in (0, 1):
            B = "B%d" % (2 + hf); key = ("key", hf); H = h_(hf); N_ = ap(B, s_(384, 512))
            energy("gcd", "mF", hf, False)
            V("tt", [key, ("keyS", hf)], [("tk", hf)], 128, [B], ap("tk", H), ap(B, s_(0, 128)), ap("keyS", H), A.is_lt)
            V("tt", [("e1", hf), ("tk", hf)], [("tm", hf)], 128, [B], ap("tm", H), ap(B, s_(256, 384)), ap("tk", H), A.mult)
            M([("Lh", hf), "Ih"], [("np", hf)], B, N_, ap("Ih"), ap("Lh", H), True, False, 128, 128, more=True)
            M([("tm", hf), "Ih"], [("np", hf)], B, N_, ap("tm", H), ap("Ih"), False, True, 128, 128)
            either([("np", hf)], [("w2", hf)], 128, ap("w2", H), N_, [B])
            src = ind("w2", 0, 512, "uS", 8 * hf, 8 * hf + 8); rr = [("w2", 0), ("w2", 1), "w2f", ("uS", hf)]
            if st < 2:
                nm = "%d%d" % (st + 1, hf)
                V("copy", rr, [("snd", nm)], gcost(128), [], ap("snd" + nm), src)
                op("g", nm, [("snd", nm)], [("in", st + 1, hf)], 300, kind="r", lat=LINK, sem="a" + nm)
            else:
                either(rr, [("outf", hf)], gcost(128), ap("outf", H), src)
                D("y", ap("yl", H), ap("outf", H), [("outf", hf)], [("yl", hf)], 2200)
    return ops


def schedule(ops):
    n = len(ops)
    pred = [sorted(o["hard"] | o["soft"]) for o in ops]
    anc = [0] * n
    for i in range(n):
        far = 0
        for j in pred[i]:
            if j in ops[i]["hard"]: far |= anc[j]
        for j in pred[i]: anc[i] |= anc[j] | (1 << j)
        pred[i] = [j for j in pred[i] if not (far >> j) & 1 or ops[j]["kind"] != "c"]
    succ = [[] for _ in range(n)]
    for i in range(n):
        for j in pred[i]: succ[j].append(i)
    hard = [[j in ops[i]["hard"] for j in pred[i]] for i in range(n)]
    hs = [[j in ops[k]["hard"] for k in succ[j]] for j in range(n)]
    cost = [[float(o["cost"][c]) for o in ops] for c in range(3)]
    lat = [[float(o["lat"][c]) for o in ops] for c in range(3)]
    LA = [float(x) for x in LAT]; SL = [float(x) for x in SLAT]
    def ready(i, fin, eng, c):
        t = 0.0; e = eng[i]; lc = lat[c]
        for j, h in zip(pred[i], hard[i]):
            u = fin[j] + lc[j] + (SL[c] if eng[j] == e else LA[c]) if h else fin[j]
            if u > t: t = u
        return t
    def sgs(key, eng, back=False):
        P_, S_ = (succ, pred) if back else (pred, succ)
        left = [len(p) for p in P_]; cand = sorted((key[i], i) for i in range(n) if left[i] == 0)
        fin = [0.0] * n; busy = {}; c0 = cost[0]; l0 = lat[0]
        while cand:
            i = cand.pop()[1]
            if back:
                t = l0[i]; e = eng[i]
                for k, h in zip(succ[i], hs[i]):
                    u = fin[k] + l0[i] + (SL[0] if eng[k] == e else LA[0]) if h else fin[k]
                    if u > t: t = u
            else: t = ready(i, fin, eng, 0)
            c = c0[i]; iv = busy.setdefault(eng[i], []); p = len(iv)
            while p > 0 and iv[p - 1][1] > t: p -= 1
            while p < len(iv) and iv[p][0] < t + c:
                t = max(t, iv[p][1]); p += 1
            iv.insert(p, (t, t + c)); fin[i] = t + c
            for k in S_[i]:
                left[k] -= 1
                if left[k] == 0: cand.append((key[k], k)); cand.sort()
        if back: return fin
        return sorted(range(n), key=lambda i: (fin[i] - c0[i], i))
    def replay(order, eng, c):
        fin = [0.0] * n; free = {}
        for i in order:
            fin[i] = free[eng[i]] = max(ready(i, fin, eng, c), free.get(eng[i], 0.0)) + cost[c][i]
        return fin
    def rate(order, eng):
        return [max(f + l for f, l in zip(replay(order, eng, c), lat[c])) for c in range(3)]
    def blocked(order, eng, c):
        fin = replay(order, eng, c); prev = {}; lastq = {}
        for i in order:
            prev[i] = lastq.get(eng[i]); lastq[eng[i]] = i
        i = max(range(n), key=lambda x: fin[x] + lat[c][x]); out = []
        while True:
            t = ready(i, fin, eng, c); p = prev[i]
            if p is not None and fin[p] > t + 1e-6:
                if p not in pred[i]: out.append((p, i))
                i = p
            elif pred[i]:
                i = max(zip(pred[i], hard[i]), key=lambda x: fin[x[0]] + (lat[c][x[0]] + (SL[c] if eng[x[0]] == eng[i] else LA[c]) if x[1] else 0.0))[0]
            else: return out
    def push(k, i, v, nb, sg):
        st = [(i, v)]
        while st:
            j, u = st.pop()
            if sg * (k[j] - u) < 0:
                k[j] = u; st.extend((x, u + sg) for x in nb[j])
    def flip(e): return "v" if e == "s" else "s"
    rng = np.random.RandomState(SEED)
    eng = [o["eng"] for o in ops]; flex = [i for i in range(n) if ops[i]["alt"]]
    twin = {}; cnt = {}
    for i, o in enumerate(ops):
        w0 = o["w"][0]; nm = (o["eng"], w0 if isinstance(w0, str) else w0[0]); c = cnt.get((nm, o["st"]), 0); cnt[(nm, o["st"])] = c + 1
        twin.setdefault((nm, c, o["st"] < 0), []).append(i)
    tw = {i: l for l in twin.values() for i in l}
    key = [0.0] * n
    for i in range(n - 1, -1, -1):
        key[i] = cost[0][i] + lat[0][i] + max([LA[0] + key[k] for k in succ[i]] + [0.0])
    order = sgs(key, eng); r = rate(order, eng); now = sum(r); top = (now, order, eng, r); blk = blocked(order, eng, 0)
    for it in range(TRIES):
        k2 = list(key); e2 = list(eng); u = rng.rand(); tied = rng.rand() < 0.7
        if rng.rand() < CP and blk:
            p, i = blk[rng.randint(len(blk))]
            prs = list(zip(tw[p], tw[i])) if tied and len(tw[p]) == len(tw[i]) and ops[p]["st"] == ops[i]["st"] else [(p, i)]
            for p, i in prs:
                if u < 0.3 and ops[p]["alt"]: e2[p] = flip(e2[p])
                elif u < 0.45 and ops[i]["alt"]: e2[i] = flip(e2[i])
                elif u < 0.7: push(k2, i, k2[p] + 1 + 1000 * u * rng.rand(), pred, 1)
                else: push(k2, p, k2[i] - 1 - 2000 * rng.rand(), succ, -1)
        elif u < 0.3:
            for i in rng.choice(flex, rng.randint(1, 3)):
                e = flip(e2[i])
                for j in (tw[i] if tied else [i]):
                    if ops[j]["alt"]: e2[j] = e
        elif u < 0.75:
            a = rng.randint(n); d = rng.randn() * 2500
            for i in range(a, min(n, a + rng.randint(1, 20))):
                for j in (tw[i] if tied else [i]): k2[j] += d
        else:
            for i in rng.randint(0, n, 6):
                d = rng.randn() * 1500
                for j in (tw[i] if tied else [i]): k2[j] += d
        o2 = sgs(k2, e2)
        if rng.rand() < FB:
            k2 = sgs(replay(o2, e2, 0), e2, True); o2 = sgs(k2, e2)
        r2 = rate(o2, e2)
        if sum(r2) <= now + TEMP * (1 - it / TRIES):
            key, eng, now = k2, e2, sum(r2); blk = blocked(o2, e2, rng.randint(3))
            if now < top[0]: top = (now, o2, e2, r2)
    now, order, eng, r = top
    for i in flex:
        if eng[i] == "v": ops[i]["eng"] = "v"; ops[i]["fn"] = ops[i]["alt"]
    CACHE["r"] = r
    return order, replay(order, eng, 0)


def plan():
    if "p" not in CACHE:
        ops = build(); order, fin = schedule(ops)
        pos = {i: p for p, i in enumerate(order)}
        seen = {}; waits = {}; need = set()
        for i in order:
            o = ops[i]; w = []; last = {}
            for j in o["hard"]:
                d = ops[j]
                if d["kind"] == "c":
                    if d["eng"] not in last or pos[j] > pos[last[d["eng"]]]: last[d["eng"]] = j
                elif (o["eng"], j) not in seen:
                    seen[(o["eng"], j)] = 1; w.append(j)
            for e, j in last.items():
                if seen.get((o["eng"], e), -1) < pos[j]:
                    seen[(o["eng"], e)] = pos[j]; w.append(j); need.add(j)
            waits[i] = w
        cnt = {}; val = {}
        for i in order:
            if i in need:
                e = ops[i]["eng"]; cnt[e] = cnt.get(e, 0) + 1; val[i] = cnt[e]
        CACHE["p"] = (ops, order, waits, val, fin)
    return CACHE["p"]


def ring_engines(topo, src, dst):
    e = topo.engines(src, dst)
    return e[::2] if len(e) > 8 else e


def rank_program(g, core, T, topo):
    rank = T.rank_of(core)
    if rank is None:
        return
    n = len(T.cores)
    nxt, prv = T.cores[(rank + 1) % n], T.cores[(rank - 1) % n]
    rid, pid = topo.addr(nxt, core)
    eo = ring_engines(topo, core, nxt); mask = sum(1 << e for e in eo); nin = len(ring_engines(topo, prv, core))
    ops, order, waits, val, fin = plan()
    Q = {"v": g.vector, "s": g.scalar, "t": g.tensor, "g": g, "y": g.sync}
    sent = 0
    for i in order:
        o = ops[i]; q = Q[o["eng"]]
        for j in waits[i]:
            d = ops[j]
            if d["kind"] == "c": q.wait_ge(T.sem[SEM[d["eng"]]], val[j])
            else: q.wait_ge(T.sem[d["sem"]], 16 if d["kind"] == "d" else nin)
        if o["kind"] == "r":
            g.remote_dma(T["in" + o["fn"]][:], T["snd" + o["fn"]][:], T.sem[o["sem"]], T.sem.sent, pid, rid, mask); sent += len(eo)
        elif o["kind"] == "d":
            o["fn"](g, T).then_inc(T.sem[o["sem"]], 16)
        else:
            ins = o["fn"](g, T)
            if i in val: ins.then_inc(T.sem[SEM[o["eng"]]], 1)
    g.wait_ge(T.sem.sent, sent)
    for o in ops:
        if o["kind"] == "d": g.wait_ge(T.sem[o["sem"]], 16)
